import numpy as np
import ml_dtypes


def mxq(x, axis, fmt="e4m3"):
    dtype, down = {"e4m3": (ml_dtypes.float8_e4m3fn, 7), "e5m2": (ml_dtypes.float8_e5m2, 14)}[fmt]
    v = np.moveaxis(np.asarray(x, np.float32).astype(ml_dtypes.bfloat16).astype(np.float64), axis, -1)
    blocks = v.reshape(v.shape[:-1] + (-1, 32))
    amax = np.abs(blocks).max(-1, keepdims=True)
    byte = np.maximum(np.where(amax > 0, np.frexp(amax)[1] - 1 + 127, 0) - down, 1)
    scale = np.exp2(byte - 127.0)
    codes = (blocks / scale).astype(np.float32).astype(dtype).astype(np.float64)
    return np.moveaxis((codes * scale).reshape(v.shape), -1, axis)


WIDE = False


def mx_kscale(k):
    if not WIDE:
        return np.ones(k)
    levels = np.array([10, -10, 5, -5, 0])
    if k % 512:
        return np.exp2(np.random.permutation(np.resize(levels, k // 32))).repeat(32)
    a = np.empty((k // 512, 16))
    for p in range(k // 512):
        a[p, :8] = np.random.permutation(np.resize(levels, 8))
        for g in range(8):
            far = levels[np.abs(levels - a[p, g]) >= 10]
            a[p, g + 8] = far[np.random.randint(len(far))]
    return np.exp2(a.ravel()).repeat(32)


def f64(x):
    return np.asarray(x).astype(np.float64)


def striped8(idx):
    return np.asarray(idx).reshape(8, -1, 16).transpose(0, 2, 1).reshape(128, -1).astype(np.uint16)


def unstriped8(offs):
    return offs.reshape(8, 16, -1).transpose(0, 2, 1).reshape(8, -1).astype(np.int64)


def pick8(x, idx, run):
    r = np.arange(len(x))
    return x[r[:, None], idx[r % (8 * run) // run]]


E2M1 = np.array([0.0, 0.5, 1.0, 1.5, 2.0, 3.0, 4.0, 6.0, -0.0, -0.5, -1.0, -1.5, -2.0, -3.0, -4.0, -6.0])


def pack_weight(w, fmt):
    k, n = w.shape
    w = f64(np.asarray(w, np.float32).astype(ml_dtypes.bfloat16)).reshape(k // 32, 32, n)
    amax = np.abs(w).max(1)
    if fmt == "e4m3":
        byte = np.frexp(amax)[1] - 1 + 127 - 7
    else:
        mant, ex = np.frexp(amax / 6.0)
        byte = np.where(mant > 0.5, ex, ex - 1) + 127
    byte = np.clip(np.where(amax > 0, byte, 1), 1, 254)
    scaled = (w * np.exp2(127.0 - byte)[:, None, :]).reshape(k, n).astype(np.float32)
    by_word = np.ascontiguousarray(scaled.reshape(k // 512, 128, 4, n).transpose(0, 1, 3, 2))
    if fmt == "e4m3":
        words = by_word.astype(ml_dtypes.float8_e4m3fn).view(np.uint8)
    else:
        c = by_word.astype(ml_dtypes.float4_e2m1fn).view(np.uint8) & 0xF
        words = (c[..., 0::2] | (c[..., 1::2] << 4)).reshape(k // 512, 128, 2 * n)
    return np.ascontiguousarray(words), np.ascontiguousarray(byte.astype(np.uint8).reshape(k // 512, 16, n))


def unpack_weight(words, scales, fmt):
    g, _, n = scales.shape
    words = np.ascontiguousarray(words).reshape(g, 128, n, -1)
    if fmt == "e4m3":
        vals = words.view(ml_dtypes.float8_e4m3fn).astype(np.float64)
    else:
        nib = np.empty((g, 128, n, 4), np.uint8)
        nib[..., 0::2] = words & 0xF
        nib[..., 1::2] = words >> 4
        vals = E2M1[nib]
    vals = vals * np.repeat(np.exp2(scales.astype(np.float64) - 127.0), 8, axis=1)[..., None]
    return vals.transpose(0, 1, 3, 2).reshape(g * 512, n)


D, E, T, Q, I = 512, 512, 1024, 128, 512


def setup_inputs():
    n = np.random.standard_normal
    idx = np.stack([np.random.permutation(T)[:I] for _ in range(8)])
    idx2 = np.stack([np.random.permutation(T)[:I] for _ in range(8)])
    fd = mx_kscale(D)
    fe = mx_kscale(E)
    keysp = pack_weight(n((D, T)) / fd[:, None], "e2m1")
    return {
        "query": (n((D, Q)) * 0.7 / np.sqrt(D) * fd[:, None]).astype(np.float32),
        "keys_words": keysp[0],
        "keys_scales": keysp[1],
        "gout": (n((E, Q)) * 1 / np.sqrt(E) * fe[:, None]).astype(np.float32),
        "vals": (n((E, T)) / fe[:, None]).astype(np.float32),
        "dquery": (n((D, Q)) * 1.0 / np.sqrt(D) * fd[:, None]).astype(np.float32),
        "base": (0.5 * n((Q, T))).astype(np.float32),
        "offs": striped8(idx),
        "offs2": striped8(idx2),
    }


def reference(query, keys_words, keys_scales, gout, vals, dquery, base, offs, offs2):
    idx = unstriped8(offs)
    idx2 = unstriped8(offs2)
    keysu = unpack_weight(keys_words, keys_scales, "e2m1")
    queryq = mxq(f64(query), 0, "e4m3")
    a = queryq.T @ keysu
    dqueryq = mxq(f64(dquery), 0, "e4m3")
    ta = dqueryq.T @ keysu
    s = pick8(a, idx, 16) * pick8(a, idx2, 16) + (pick8(a, idx, 16) + pick8(a, idx2, 16)) * 0.5
    p = np.exp(s - np.max(s, axis=1, keepdims=True))
    z = np.sum(p, axis=1, keepdims=True)
    goutq = mxq(f64(gout), 0, "e4m3")
    valsq = mxq(f64(vals), 0, "e4m3")
    c0 = goutq.T @ valsq
    dw = pick8(c0, idx, 16)
    dz = np.sum(dw * p / np.square(z) * (-1.0), axis=1, keepdims=True)
    dp = dw / z + dz
    ds = dp * p
    xs = pick8(ta, idx, 16) * pick8(a, idx2, 16) + pick8(ta, idx2, 16) * pick8(a, idx, 16) + (pick8(ta, idx, 16) + pick8(ta, idx2, 16)) * 0.5
    xp = xs * p
    xz = np.sum(xp, axis=1, keepdims=True)
    xdz = np.sum((xp * dw - xz * z * 2.0 * dw * p / np.square(z)) / np.square(z) * (-1.0), axis=1, keepdims=True)
    xdp = xz * dw / np.square(z) * (-1.0) + xdz
    xds = xdp * p + xp * dp
    xe1 = xds * pick8(a, idx2, 16) + pick8(ta, idx2, 16) * ds
    xs1 = np.zeros((Q, T))
    xs1[np.arange(Q)[:, None], idx[np.arange(Q) % 128 // 16]] = xe1
    xe2 = xds * 0.5
    xs2 = np.zeros((Q, T))
    xs2[np.arange(Q)[:, None], idx[np.arange(Q) % 128 // 16]] = xe2
    xe3 = xds * pick8(a, idx, 16) + pick8(ta, idx, 16) * ds
    xs3 = np.zeros((Q, T))
    xs3[np.arange(Q)[:, None], idx2[np.arange(Q) % 128 // 16]] = xe3
    xe4 = xds * 0.5
    xs4 = np.zeros((Q, T))
    xs4[np.arange(Q)[:, None], idx2[np.arange(Q) % 128 // 16]] = xe4
    xda = xs1 + xs2 + xs3 + xs4
    y = xda * 512.0 + f64(base)
    return y

@@ -1,0 +1,168 @@
+from contextlib import ExitStack
+
+import concourse.mybir as mybir
+from concourse.masks import make_identity
+
+D, E, T, Q, SLOTS = 512, 512, 1024, 128, 512
+FLOPS = 3 * 2 * 512 * 128 * 1024
+
+F32 = mybir.dt.float32
+BF16 = mybir.dt.bfloat16
+I32 = mybir.dt.int32
+U32 = mybir.dt.uint32
+U16 = mybir.dt.uint16
+U8 = mybir.dt.uint8
+FP8X4 = mybir.dt.float8_e4m3fn_x4
+FP4X4 = mybir.dt.float4_e2m1fn_x4
+ALU = mybir.AluOpType
+ACT = mybir.ActivationFunctionType
+
+P = 128
+PACK = 4
+BANK = 512
+CHUNK = 256
+OUT_SCALE = 512.0
+
+
+def tile_attend_hvproductpairs_heads_kernel(tc, query, keys_words, keys_scales, gout, vals, dquery, base, offs, offs2, out):
+    nc = tc.nc
+    with ExitStack() as ctx:
+        sb = ctx.enter_context(tc.tile_pool(name="sb", bufs=1))
+        shared = ctx.enter_context(tc.tile_pool(name="shared", bufs=1))
+        ps = ctx.enter_context(tc.psum_pool(name="ps", bufs=1))
+
+        def load_rows(name, rows, raw=None):
+            if raw is None:
+                raw = sb.tile([P, PACK, rows.shape[1]], F32, name=name + "_raw", align_bytes=64)
+            nc.sync.dma_start(out=raw[:], in_=rows.rearrange("(p j) w -> p j w", j=PACK))
+            return raw
+
+        def interleave(name, raw, copy):
+            width = raw.shape[2]
+            grouped = sb.tile([P, width * PACK], BF16, name=name + "_bf", align_bytes=64)
+            copy(out=grouped[:].rearrange("p (c i j) -> p c j i", i=4, j=PACK),
+                 in_=raw[:].rearrange("p j (c i) -> p c j i", i=4))
+            return grouped
+
+        def quantize(name, grouped):
+            width = grouped.shape[1] // PACK
+            codes = sb.tile([P, width], U32, name=name + "_codes", align_bytes=64)
+            scales = sb.tile([P, width], U8, name=name + "_scales", align_bytes=64)
+            nc.vector.quantize_mx(out=codes[:].bitcast(FP8X4), scales=scales[:], in_=grouped[:])
+            return codes, scales
+
+        def wide(name, on=None):
+            return sb.tile([P, SLOTS], F32, name=name, tag=on or name, align_bytes=64)
+
+        def column(name):
+            return sb.tile([P, 1], F32, name=name)
+
+        k_scales = sb.tile([P, T], U8, name="k_scales", align_bytes=64)
+        nc.vector.memset(k_scales[:].bitcast(U32), 0)
+        q_raw = load_rows("q", query)
+        k_words = sb.tile([P, 2 * T], U8, name="k_words", align_bytes=64)
+        nc.sync.dma_start(out=k_words[:].bitcast(I32), in_=keys_words[0].bitcast(I32))
+        for quad in range(4):
+            nc.sync.dma_start(out=k_scales[32 * quad:32 * quad + 4, :].bitcast(I32),
+                              in_=keys_scales[0, 4 * quad:4 * quad + 4, :].bitcast(I32))
+        list1 = sb.tile([P, SLOTS // 16], U16, name="list1")
+        nc.sync.dma_start(list1[:], offs)
+        dq_raw = load_rows("dq", dquery)
+        list2 = sb.tile([P, SLOTS // 16], U16, name="list2")
+        nc.sync.dma_start(list2[:], offs2)
+        g_raw = load_rows("g", gout)
+        v_raw = [load_rows("v%d" % c, vals[:, c * CHUNK:(c + 1) * CHUNK]) for c in range(T // CHUNK - 1)]
+        v_last = shared.tile([P, PACK, CHUNK], F32, name="v_last", offset=0)
+        v_raw.append(load_rows("v3", vals[:, T - CHUNK:T], v_last))
+        base_sb = sb.tile([P, T], F32, name="base_sb")
+        nc.sync.dma_start(out=base_sb[:], in_=base)
+
+        placed1 = sb.tile([P, T], F32, name="placed1")
+        placed2 = sb.tile([P, T], F32, name="placed2")
+        nc.vector.memset(placed1[:], 0.0)
+        nc.vector.memset(placed2[:], 0.0)
+        ident = sb.tile([P, P], F32, name="ident")
+        make_identity(nc, ident[:])
+
+        def score_keys(name, codes, scales, width, copies):
+            whole = sb.tile([P, T], F32, name=name)
+            for h in range(T // width):
+                bank = ps.tile([P, width], F32, name="%s_bank%d" % (name, h))
+                nc.tensor.matmul_mx(out=bank[:], lhsT=codes[:].bitcast(FP8X4), lhsT_scale=scales[:],
+                                    rhs=k_words[:, 2 * width * h:2 * width * (h + 1)].bitcast(FP4X4),
+                                    rhs_scale=k_scales[:, width * h:width * (h + 1)], start=True, stop=True)
+                copies[h % len(copies)](out=whole[:, width * h:width * (h + 1)], in_=bank[:])
+            return whole
+
+        q_codes, q_scales = quantize("q", interleave("q", q_raw, nc.vector.tensor_copy))
+        a = score_keys("a", q_codes, q_scales, CHUNK, [nc.scalar.copy, nc.vector.tensor_copy])
+        dq_codes, dq_scales = quantize("dq", interleave("dq", dq_raw, nc.vector.tensor_copy))
+        ta = score_keys("ta", dq_codes, dq_scales, BANK, [nc.scalar.copy])
+        g_codes, g_scales = quantize("g", interleave("g", g_raw, nc.vector.tensor_copy))
+
+        u1, u2, s, t1, t2 = wide("u1"), wide("u2"), wide("s"), wide("t1"), wide("t2")
+        neg_max, z, rz, r_out, neg_r_out = column("neg_max"), column("z"), column("rz"), column("r_out"), column("neg_r_out")
+        nc.vector.tensor_scalar(u1[:], a[:].indirect(list1[:]), 1.0, 0.5, ALU.mult, ALU.add)
+        nc.vector.tensor_scalar(u2[:], a[:].indirect(list2[:]), 1.0, 0.5, ALU.mult, ALU.add)
+        nc.vector.tensor_copy(t1[:], ta[:].indirect(list1[:]))
+        nc.vector.tensor_tensor(s[:], u1[:], u2[:], ALU.mult)
+        nc.vector.tensor_copy(t2[:], ta[:].indirect(list2[:]))
+        nc.vector.tensor_reduce(neg_max[:], s[:], mybir.AxisListType.X, ALU.max, negate=True)
+
+        chunks = T // CHUNK
+        v_bf = [interleave("v%d" % c, v_raw[c], nc.scalar.copy) for c in range(chunks)]
+        p = shared.tile([P, SLOTS], F32, name="p", offset=0)
+        nc.scalar.activation(p[:], s[:], ACT.Exp, bias=neg_max[:], scale=1.0, accum_out=z[:])
+        nc.vector.reciprocal(rz[:], z[:])
+        nc.scalar.activation(r_out[:], rz[:], ACT.Copy, scale=OUT_SCALE)
+        nc.scalar.activation(neg_r_out[:], rz[:], ACT.Copy, scale=-OUT_SCALE)
+
+        c0 = shared.tile([P, T], F32, name="c0", offset=4 * SLOTS)
+        for c in range(chunks):
+            v_codes, v_scales = quantize("v%d" % c, v_bf[c])
+            bank = ps.tile([P, CHUNK], F32, name="c0_bank%d" % c, tag="a_bank%d" % c)
+            nc.tensor.matmul_mx(out=bank[:], lhsT=g_codes[:].bitcast(FP8X4), lhsT_scale=g_scales[:],
+                                rhs=v_codes[:].bitcast(FP8X4), rhs_scale=v_scales[:], start=True, stop=True)
+            nc.scalar.copy(out=c0[:, CHUNK * c:CHUNK * (c + 1)], in_=bank[:])
+
+        x2, x1, xs = wide("x2", on="v3_bf"), wide("x1", on="v3_codes"), wide("xs")
+        nc.vector.tensor_tensor(x2[:], t2[:], u1[:], ALU.mult)
+        nc.vector.tensor_tensor(x1[:], t1[:], u2[:], ALU.mult)
+
+        pdw, wdw, wxs = wide("pdw"), wide("wdw"), wide("wxs")
+        m, mx, neg_zcov = column("m"), column("mx"), column("neg_zcov")
+        nc.vector.tensor_tensor(pdw[:], c0[:].indirect(list1[:]), p[:], ALU.mult)
+        nc.scalar.activation(wdw[:], pdw[:], ACT.Copy, scale=rz[:], accum_out=m[:])
+        nc.vector.tensor_tensor(xs[:], x1[:], x2[:], ALU.add)
+        nc.vector.scalar_tensor_tensor(wxs[:], xs[:], rz[:], p[:], ALU.mult, ALU.mult, accum_out=mx[:])
+        w = shared.tile([P, SLOTS], F32, name="w", offset=4 * SLOTS)
+        nc.scalar.activation(w[:], p[:], ACT.Copy, scale=rz[:])
+
+        neg_ds, neg_c, xds = wide("neg_ds"), wide("neg_c"), wide("xds")
+        nc.vector.scalar_tensor_tensor(neg_ds[:], p[:], m[:], pdw[:], ALU.mult, ALU.subtract)
+        nc.vector.scalar_tensor_tensor(neg_c[:], xs[:], mx[:], neg_ds[:], ALU.subtract, ALU.mult, accum_out=neg_zcov[:])
+        y1, y2, y3, y4 = wide("y1"), wide("y2"), wide("y3"), wide("y4")
+        nc.vector.scalar_tensor_tensor(y2[:], neg_ds[:], neg_r_out[:], t2[:], ALU.mult, ALU.mult)
+        nc.vector.scalar_tensor_tensor(xds[:], w[:], neg_zcov[:], neg_c[:], ALU.mult, ALU.subtract)
+        nc.vector.scalar_tensor_tensor(y4[:], neg_ds[:], neg_r_out[:], t1[:], ALU.mult, ALU.mult)
+        nc.vector.scalar_tensor_tensor(y1[:], xds[:], r_out[:], u2[:], ALU.mult, ALU.mult)
+        nc.vector.scalar_tensor_tensor(y3[:], xds[:], r_out[:], u1[:], ALU.mult, ALU.mult)
+        nc.vector.tensor_tensor(placed1[:].indirect(list1[:]), y1[:], y2[:], ALU.add)
+        nc.vector.tensor_tensor(placed2[:].indirect(list2[:]), y3[:], y4[:], ALU.add)
+
+        blocks = BANK // P
+        for h in range(T // BANK):
+            turned = ps.tile([P, BANK], F32, name="turned%d" % h, tag="ta_bank%d" % h)
+            for i, src in enumerate((base_sb, placed1)):
+                for b in range(blocks):
+                    lo = BANK * h + P * b
+                    nc.tensor.matmul(turned[:, P * b:P * (b + 1)], src[:, lo:lo + P], ident[:], is_transpose=True,
+                                     start=(i == 0 and b == 0), stop=(i == 1 and b == blocks - 1))
+            turned_sb = sb.tile([P, BANK], F32, name="turned_sb%d" % h)
+            nc.scalar.copy(out=turned_sb[:], in_=turned[:])
+            back = ps.tile([P, BANK], F32, name="back%d" % h)
+            for b in range(blocks):
+                nc.tensor.transpose(back[:, P * b:P * (b + 1)], turned_sb[:, P * b:P * (b + 1)], ident[:])
+            result = sb.tile([P, BANK], F32, name="result%d" % h)
+            nc.vector.tensor_tensor(result[:], back[:], placed2[:, BANK * h:BANK * (h + 1)], ALU.add)
+            nc.sync.dma_start(out=out[:, BANK * h:BANK * (h + 1)], in_=result[:])

@@ -58,19 +58,19 @@ def tile_attend_hvproductpairs_heads_kernel(tc, query, keys_words, keys_scales, 
             return sb.tile([P, 1], F32, name=name)
 
         k_scales = sb.tile([P, T], U8, name="k_scales", align_bytes=64)
-        nc.vector.memset(k_scales[:].bitcast(U32), 0)
+        nc.gpsimd.memset(k_scales[:].bitcast(U32), 0)
         q_raw = load_rows("q", query)
         k_words = sb.tile([P, 2 * T], U8, name="k_words", align_bytes=64)
         nc.sync.dma_start(out=k_words[:].bitcast(I32), in_=keys_words[0].bitcast(I32))
         for quad in range(4):
             nc.sync.dma_start(out=k_scales[32 * quad:32 * quad + 4, :].bitcast(I32),
                               in_=keys_scales[0, 4 * quad:4 * quad + 4, :].bitcast(I32))
+        dq_raw = load_rows("dq", dquery)
+        g_raw = load_rows("g", gout)
         list1 = sb.tile([P, SLOTS // 16], U16, name="list1")
         nc.sync.dma_start(list1[:], offs)
-        dq_raw = load_rows("dq", dquery)
         list2 = sb.tile([P, SLOTS // 16], U16, name="list2")
         nc.sync.dma_start(list2[:], offs2)
-        g_raw = load_rows("g", gout)
         v_raw = [load_rows("v%d" % c, vals[:, c * CHUNK:(c + 1) * CHUNK]) for c in range(T // CHUNK - 1)]
         v_last = shared.tile([P, PACK, CHUNK], F32, name="v_last", offset=0)
         v_raw.append(load_rows("v3", vals[:, T - CHUNK:T], v_last))
@@ -95,7 +95,7 @@ def tile_attend_hvproductpairs_heads_kernel(tc, query, keys_words, keys_scales, 
             return whole
 
         q_codes, q_scales = quantize("q", interleave("q", q_raw, nc.vector.tensor_copy))
-        a = score_keys("a", q_codes, q_scales, CHUNK, [nc.scalar.copy, nc.vector.tensor_copy])
+        a = score_keys("a", q_codes, q_scales, CHUNK, [nc.scalar.copy])
         dq_codes, dq_scales = quantize("dq", interleave("dq", dq_raw, nc.vector.tensor_copy))
         ta = score_keys("ta", dq_codes, dq_scales, BANK, [nc.scalar.copy])
         g_codes, g_scales = quantize("g", interleave("g", g_raw, nc.vector.tensor_copy))
@@ -105,12 +105,17 @@ def tile_attend_hvproductpairs_heads_kernel(tc, query, keys_words, keys_scales, 
         nc.vector.tensor_scalar(u1[:], a[:].indirect(list1[:]), 1.0, 0.5, ALU.mult, ALU.add)
         nc.vector.tensor_scalar(u2[:], a[:].indirect(list2[:]), 1.0, 0.5, ALU.mult, ALU.add)
         nc.vector.tensor_copy(t1[:], ta[:].indirect(list1[:]))
-        nc.vector.tensor_tensor(s[:], u1[:], u2[:], ALU.mult)
         nc.vector.tensor_copy(t2[:], ta[:].indirect(list2[:]))
+        v_first = sb.tile([P, CHUNK * PACK], BF16, name="v0_bf", align_bytes=64)
+        nc.gpsimd.tensor_scalar(v_first[:].rearrange("p (w j) -> p w j", j=PACK), v_raw[0][:].rearrange("p j w -> p w j"),
+                                1.0, 0.0, ALU.mult, ALU.add)
+        x1 = wide("x1")
+        nc.gpsimd.tensor_tensor(s[:], u1[:], u2[:], ALU.mult)
+        nc.gpsimd.tensor_tensor(x1[:], t1[:], u2[:], ALU.mult)
         nc.vector.tensor_reduce(neg_max[:], s[:], mybir.AxisListType.X, ALU.max, negate=True)
 
         chunks = T // CHUNK
-        v_bf = [interleave("v%d" % c, v_raw[c], nc.scalar.copy) for c in range(chunks)]
+        v_bf = [v_first] + [interleave("v%d" % c, v_raw[c], nc.scalar.copy) for c in range(1, chunks)]
         p = shared.tile([P, SLOTS], F32, name="p", offset=0)
         nc.scalar.activation(p[:], s[:], ACT.Exp, bias=neg_max[:], scale=1.0, accum_out=z[:])
         nc.vector.reciprocal(rz[:], z[:])
@@ -125,15 +130,14 @@ def tile_attend_hvproductpairs_heads_kernel(tc, query, keys_words, keys_scales, 
                                 rhs=v_codes[:].bitcast(FP8X4), rhs_scale=v_scales[:], start=True, stop=True)
             nc.scalar.copy(out=c0[:, CHUNK * c:CHUNK * (c + 1)], in_=bank[:])
 
-        x2, x1, xs = wide("x2", on="v3_bf"), wide("x1", on="v3_codes"), wide("xs")
+        x2, xs = wide("x2", on="v3_bf"), wide("xs")
         nc.vector.tensor_tensor(x2[:], t2[:], u1[:], ALU.mult)
-        nc.vector.tensor_tensor(x1[:], t1[:], u2[:], ALU.mult)
+        nc.vector.tensor_tensor(xs[:], x1[:], x2[:], ALU.add)
 
         pdw, wdw, wxs = wide("pdw"), wide("wdw"), wide("wxs")
         m, mx, neg_zcov = column("m"), column("mx"), column("neg_zcov")
         nc.vector.tensor_tensor(pdw[:], c0[:].indirect(list1[:]), p[:], ALU.mult)
         nc.scalar.activation(wdw[:], pdw[:], ACT.Copy, scale=rz[:], accum_out=m[:])
-        nc.vector.tensor_tensor(xs[:], x1[:], x2[:], ALU.add)
         nc.vector.scalar_tensor_tensor(wxs[:], xs[:], rz[:], p[:], ALU.mult, ALU.mult, accum_out=mx[:])
         w = shared.tile([P, SLOTS], F32, name="w", offset=4 * SLOTS)
         nc.scalar.activation(w[:], p[:], ACT.Copy, scale=rz[:])

@@ -37,11 +37,14 @@ def tile_attend_hvproductpairs_heads_kernel(tc, query, keys_words, keys_scales, 
             nc.sync.dma_start(out=raw[:], in_=rows.rearrange("(p j) w -> p j w", j=PACK))
             return raw
 
+        def weave(copy, grouped, raw):
+            copy(out=grouped.rearrange("p (c i j) -> p c j i", i=4, j=PACK),
+                 in_=raw.rearrange("p j (c i) -> p c j i", i=4))
+
         def interleave(name, raw, copy):
             width = raw.shape[2]
             grouped = sb.tile([P, width * PACK], BF16, name=name + "_bf", align_bytes=64)
-            copy(out=grouped[:].rearrange("p (c i j) -> p c j i", i=4, j=PACK),
-                 in_=raw[:].rearrange("p j (c i) -> p c j i", i=4))
+            weave(copy, grouped[:], raw[:])
             return grouped
 
         def quantize(name, grouped):
@@ -71,16 +74,17 @@ def tile_attend_hvproductpairs_heads_kernel(tc, query, keys_words, keys_scales, 
         nc.sync.dma_start(list1[:], offs)
         list2 = sb.tile([P, SLOTS // 16], U16, name="list2")
         nc.sync.dma_start(list2[:], offs2)
-        v_raw = [load_rows("v%d" % c, vals[:, c * CHUNK:(c + 1) * CHUNK]) for c in range(T // CHUNK - 1)]
-        v_last = shared.tile([P, PACK, CHUNK], F32, name="v_last", offset=0)
-        v_raw.append(load_rows("v3", vals[:, T - CHUNK:T], v_last))
+        v_cols = [(0, 256), (256, 512), (512, 768), (768, 896), (896, 1024)]
+        v_raw = [load_rows("v%d" % c, vals[:, lo:hi]) for c, (lo, hi) in enumerate(v_cols[:-1])]
+        v_last = shared.tile([P, PACK, P], F32, name="v_last", offset=2 * SLOTS)
+        v_raw.append(load_rows("v4", vals[:, T - P:T], v_last))
         base_sb = sb.tile([P, T], F32, name="base_sb")
         nc.sync.dma_start(out=base_sb[:], in_=base)
 
         placed1 = sb.tile([P, T], F32, name="placed1")
         placed2 = sb.tile([P, T], F32, name="placed2")
         nc.vector.memset(placed1[:], 0.0)
-        nc.vector.memset(placed2[:], 0.0)
+        nc.gpsimd.memset(placed2[:], 0.0)
         ident = sb.tile([P, P], F32, name="ident")
         make_identity(nc, ident[:])
 
@@ -94,63 +98,77 @@ def tile_attend_hvproductpairs_heads_kernel(tc, query, keys_words, keys_scales, 
                 copies[h % len(copies)](out=whole[:, width * h:width * (h + 1)], in_=bank[:])
             return whole
 
-        q_codes, q_scales = quantize("q", interleave("q", q_raw, nc.vector.tensor_copy))
+        q_bf = sb.tile([P, Q * PACK], BF16, name="q_bf", align_bytes=64)
+        q_codes = sb.tile([P, Q], U32, name="q_codes", align_bytes=64)
+        q_scales = sb.tile([P, Q], U8, name="q_scales", align_bytes=64)
+        halves = [(0, Q // 2), (Q // 2, Q)]
+        for lo, hi in halves:
+            weave(nc.vector.tensor_copy, q_bf[:, PACK * lo:PACK * hi], q_raw[:, :, lo:hi])
+        for lo, hi in halves:
+            nc.vector.quantize_mx(out=q_codes[:, lo:hi].bitcast(FP8X4), scales=q_scales[:, lo:hi], in_=q_bf[:, PACK * lo:PACK * hi])
         a = score_keys("a", q_codes, q_scales, CHUNK, [nc.scalar.copy])
         dq_codes, dq_scales = quantize("dq", interleave("dq", dq_raw, nc.vector.tensor_copy))
         ta = score_keys("ta", dq_codes, dq_scales, BANK, [nc.scalar.copy])
         g_codes, g_scales = quantize("g", interleave("g", g_raw, nc.vector.tensor_copy))
 
         u1, u2, s, t1, t2 = wide("u1"), wide("u2"), wide("s"), wide("t1"), wide("t2")
-        neg_max, z, rz, r_out, neg_r_out = column("neg_max"), column("z"), column("rz"), column("r_out"), column("neg_r_out")
+        neg_max, z, rz, neg_r = column("neg_max"), column("z"), column("rz"), column("neg_r")
         nc.vector.tensor_scalar(u1[:], a[:].indirect(list1[:]), 1.0, 0.5, ALU.mult, ALU.add)
         nc.vector.tensor_scalar(u2[:], a[:].indirect(list2[:]), 1.0, 0.5, ALU.mult, ALU.add)
         nc.vector.tensor_copy(t1[:], ta[:].indirect(list1[:]))
         nc.vector.tensor_copy(t2[:], ta[:].indirect(list2[:]))
-        v_first = sb.tile([P, CHUNK * PACK], BF16, name="v0_bf", align_bytes=64)
-        nc.gpsimd.tensor_scalar(v_first[:].rearrange("p (w j) -> p w j", j=PACK), v_raw[0][:].rearrange("p j w -> p w j"),
-                                1.0, 0.0, ALU.mult, ALU.add)
+        v_first = sb.tile([P, BANK * PACK], BF16, name="v_first", tag="g_bf", align_bytes=64)
+        nc.gpsimd.tensor_scalar(v_first[:, :CHUNK * PACK].rearrange("p (w j) -> p w j", j=PACK),
+                                v_raw[0][:].rearrange("p j w -> p w j"), 1.0, 0.0, ALU.mult, ALU.add)
         x1 = wide("x1")
         nc.gpsimd.tensor_tensor(s[:], u1[:], u2[:], ALU.mult)
         nc.gpsimd.tensor_tensor(x1[:], t1[:], u2[:], ALU.mult)
         nc.vector.tensor_reduce(neg_max[:], s[:], mybir.AxisListType.X, ALU.max, negate=True)
 
-        chunks = T // CHUNK
-        v_bf = [v_first] + [interleave("v%d" % c, v_raw[c], nc.scalar.copy) for c in range(1, chunks)]
+        weave(nc.scalar.copy, v_first[:, CHUNK * PACK:], v_raw[1][:])
+        v_bf = [v_first] + [interleave("v%d" % c, v_raw[c], nc.scalar.copy) for c in range(2, len(v_cols))]
         p = shared.tile([P, SLOTS], F32, name="p", offset=0)
         nc.scalar.activation(p[:], s[:], ACT.Exp, bias=neg_max[:], scale=1.0, accum_out=z[:])
         nc.vector.reciprocal(rz[:], z[:])
-        nc.scalar.activation(r_out[:], rz[:], ACT.Copy, scale=OUT_SCALE)
-        nc.scalar.activation(neg_r_out[:], rz[:], ACT.Copy, scale=-OUT_SCALE)
 
         c0 = shared.tile([P, T], F32, name="c0", offset=4 * SLOTS)
-        for c in range(chunks):
-            v_codes, v_scales = quantize("v%d" % c, v_bf[c])
-            bank = ps.tile([P, CHUNK], F32, name="c0_bank%d" % c, tag="a_bank%d" % c)
+        lo = 0
+        for c, grouped in enumerate(v_bf):
+            width = grouped.shape[1] // PACK
+            v_codes, v_scales = quantize("vq%d" % c, grouped)
+            bank = ps.tile([P, width], F32, name="c0_bank%d" % c, tag="a_bank%d" % c)
             nc.tensor.matmul_mx(out=bank[:], lhsT=g_codes[:].bitcast(FP8X4), lhsT_scale=g_scales[:],
                                 rhs=v_codes[:].bitcast(FP8X4), rhs_scale=v_scales[:], start=True, stop=True)
-            nc.scalar.copy(out=c0[:, CHUNK * c:CHUNK * (c + 1)], in_=bank[:])
+            nc.scalar.copy(out=c0[:, lo:lo + width], in_=bank[:])
+            lo = lo + width
 
-        x2, xs = wide("x2", on="v3_bf"), wide("xs")
-        nc.vector.tensor_tensor(x2[:], t2[:], u1[:], ALU.mult)
-        nc.vector.tensor_tensor(xs[:], x1[:], x2[:], ALU.add)
-
-        pdw, wdw, wxs = wide("pdw"), wide("wdw"), wide("wxs")
-        m, mx, neg_zcov = column("m"), column("mx"), column("neg_zcov")
-        nc.vector.tensor_tensor(pdw[:], c0[:].indirect(list1[:]), p[:], ALU.mult)
-        nc.scalar.activation(wdw[:], pdw[:], ACT.Copy, scale=rz[:], accum_out=m[:])
-        nc.vector.scalar_tensor_tensor(wxs[:], xs[:], rz[:], p[:], ALU.mult, ALU.mult, accum_out=mx[:])
-        w = shared.tile([P, SLOTS], F32, name="w", offset=4 * SLOTS)
+        w = wide("w", on="vq3_codes")
         nc.scalar.activation(w[:], p[:], ACT.Copy, scale=rz[:])
+        nc.scalar.activation(neg_r[:], rz[:], ACT.Copy, scale=-OUT_SCALE)
 
-        neg_ds, neg_c, xds = wide("neg_ds"), wide("neg_c"), wide("xds")
-        nc.vector.scalar_tensor_tensor(neg_ds[:], p[:], m[:], pdw[:], ALU.mult, ALU.subtract)
-        nc.vector.scalar_tensor_tensor(neg_c[:], xs[:], mx[:], neg_ds[:], ALU.subtract, ALU.mult, accum_out=neg_zcov[:])
+        x2, neg_xs = wide("x2", on="v4_bf"), wide("neg_xs")
+        nc.vector.tensor_tensor(x2[:], t2[:], u1[:], ALU.mult)
+        nc.vector.scalar_tensor_tensor(neg_xs[:], x1[:], -1.0, x2[:], ALU.mult, ALU.subtract)
+
+        pdw, neg_wdw, neg_wxs = wide("pdw"), wide("neg_wdw"), wide("neg_wxs")
+        neg_m, neg_mx, neg_cov = column("neg_m"), column("neg_mx"), column("neg_cov")
+        nc.vector.tensor_tensor(pdw[:], c0[:].indirect(list1[:]), p[:], ALU.mult)
+        nc.scalar.activation(neg_wdw[:], pdw[:], ACT.Copy, scale=neg_r[:], accum_out=neg_m[:])
+        nc.vector.scalar_tensor_tensor(neg_wxs[:], neg_xs[:], 1.0, w[:], ALU.mult, ALU.mult, accum_out=neg_mx[:])
+
+        ds, neg_c, xds = wide("ds"), wide("neg_c"), wide("xds")
         y1, y2, y3, y4 = wide("y1"), wide("y2"), wide("y3"), wide("y4")
-        nc.vector.scalar_tensor_tensor(y2[:], neg_ds[:], neg_r_out[:], t2[:], ALU.mult, ALU.mult)
-        nc.vector.scalar_tensor_tensor(xds[:], w[:], neg_zcov[:], neg_c[:], ALU.mult, ALU.subtract)
-        nc.vector.scalar_tensor_tensor(y4[:], neg_ds[:], neg_r_out[:], t1[:], ALU.mult, ALU.mult)
-        nc.vector.scalar_tensor_tensor(y1[:], xds[:], r_out[:], u2[:], ALU.mult, ALU.mult)
-        nc.vector.scalar_tensor_tensor(y3[:], xds[:], r_out[:], u1[:], ALU.mult, ALU.mult)
+        half = SLOTS // 2
+        for lo in (0, half):
+            nc.vector.scalar_tensor_tensor(ds[:, lo:lo + half], w[:, lo:lo + half], neg_m[:], neg_wdw[:, lo:lo + half],
+                                           ALU.mult, ALU.subtract)
+        nc.vector.tensor_tensor(y2[:, :half], ds[:, :half], t2[:, :half], ALU.mult)
+        nc.vector.scalar_tensor_tensor(neg_c[:], neg_xs[:], neg_mx[:], ds[:], ALU.subtract, ALU.mult, accum_out=neg_cov[:])
+        nc.vector.tensor_tensor(y2[:, half:], ds[:, half:], t2[:, half:], ALU.mult)
+        nc.vector.scalar_tensor_tensor(xds[:], w[:], neg_cov[:], neg_c[:], ALU.mult, ALU.subtract)
+        nc.vector.tensor_tensor(y4[:], ds[:], t1[:], ALU.mult)
+        nc.vector.tensor_tensor(y1[:], xds[:], u2[:], ALU.mult)
+        nc.vector.tensor_tensor(y3[:], xds[:], u1[:], ALU.mult)
         nc.vector.tensor_tensor(placed1[:].indirect(list1[:]), y1[:], y2[:], ALU.add)
         nc.vector.tensor_tensor(placed2[:].indirect(list2[:]), y3[:], y4[:], ALU.add)
 
@@ -167,6 +185,8 @@ def tile_attend_hvproductpairs_heads_kernel(tc, query, keys_words, keys_scales, 
             back = ps.tile([P, BANK], F32, name="back%d" % h)
             for b in range(blocks):
                 nc.tensor.transpose(back[:, P * b:P * (b + 1)], turned_sb[:, P * b:P * (b + 1)], ident[:])
-            result = sb.tile([P, BANK], F32, name="result%d" % h)
-            nc.vector.tensor_tensor(result[:], back[:], placed2[:, BANK * h:BANK * (h + 1)], ALU.add)
-            nc.sync.dma_start(out=out[:, BANK * h:BANK * (h + 1)], in_=result[:])
+            for lo in (0, CHUNK):
+                cols = slice(BANK * h + lo, BANK * h + lo + CHUNK)
+                result = sb.tile([P, CHUNK], F32, name="result%d" % cols.start)
+                nc.vector.tensor_tensor(result[:], back[:, lo:lo + CHUNK], placed2[:, cols], ALU.add)
+                (nc.sync if lo == 0 else nc.scalar).dma_start(out=out[:, cols], in_=result[:])

@@ -61,7 +61,7 @@ def tile_attend_hvproductpairs_heads_kernel(tc, query, keys_words, keys_scales, 
             return sb.tile([P, 1], F32, name=name)
 
         k_scales = sb.tile([P, T], U8, name="k_scales", align_bytes=64)
-        nc.gpsimd.memset(k_scales[:].bitcast(U32), 0)
+        nc.vector.memset(k_scales[:].bitcast(U32), 0)
         q_raw = load_rows("q", query)
         k_words = sb.tile([P, 2 * T], U8, name="k_words", align_bytes=64)
         nc.sync.dma_start(out=k_words[:].bitcast(I32), in_=keys_words[0].bitcast(I32))
@@ -157,7 +157,7 @@ def tile_attend_hvproductpairs_heads_kernel(tc, query, keys_words, keys_scales, 
         nc.vector.scalar_tensor_tensor(neg_wxs[:], neg_xs[:], 1.0, w[:], ALU.mult, ALU.mult, accum_out=neg_mx[:])
 
         ds, neg_c, xds = wide("ds"), wide("neg_c"), wide("xds")
-        y1, y2, y3, y4 = wide("y1"), wide("y2"), wide("y3"), wide("y4")
+        y1, y2, e1 = wide("y1"), wide("y2"), wide("e1")
         half = SLOTS // 2
         for lo in (0, half):
             nc.vector.scalar_tensor_tensor(ds[:, lo:lo + half], w[:, lo:lo + half], neg_m[:], neg_wdw[:, lo:lo + half],
@@ -165,11 +165,17 @@ def tile_attend_hvproductpairs_heads_kernel(tc, query, keys_words, keys_scales, 
         nc.vector.tensor_tensor(y2[:, :half], ds[:, :half], t2[:, :half], ALU.mult)
         nc.vector.scalar_tensor_tensor(neg_c[:], neg_xs[:], neg_mx[:], ds[:], ALU.subtract, ALU.mult, accum_out=neg_cov[:])
         nc.vector.tensor_tensor(y2[:, half:], ds[:, half:], t2[:, half:], ALU.mult)
-        nc.vector.scalar_tensor_tensor(xds[:], w[:], neg_cov[:], neg_c[:], ALU.mult, ALU.subtract)
-        nc.vector.tensor_tensor(y4[:], ds[:], t1[:], ALU.mult)
-        nc.vector.tensor_tensor(y1[:], xds[:], u2[:], ALU.mult)
-        nc.vector.tensor_tensor(y3[:], xds[:], u1[:], ALU.mult)
-        nc.vector.tensor_tensor(placed1[:].indirect(list1[:]), y1[:], y2[:], ALU.add)
+        halves = [slice(0, half), slice(half, SLOTS)]
+        for cols in halves:
+            nc.vector.scalar_tensor_tensor(xds[:, cols], w[:, cols], neg_cov[:], neg_c[:, cols], ALU.mult, ALU.subtract)
+        for cols in halves:
+            nc.vector.tensor_tensor(y1[:, cols], xds[:, cols], u2[:, cols], ALU.mult)
+        for cols in halves:
+            nc.vector.tensor_tensor(e1[:, cols], y1[:, cols], y2[:, cols], ALU.add)
+        nc.vector.tensor_copy(placed1[:].indirect(list1[:]), e1[:])
+        y3, y4 = wide("y3", on="y1"), wide("y4", on="y2")
+        nc.gpsimd.tensor_tensor(y4[:], ds[:], t1[:], ALU.mult)
+        nc.gpsimd.tensor_tensor(y3[:], xds[:], u1[:], ALU.mult)
         nc.vector.tensor_tensor(placed2[:].indirect(list2[:]), y3[:], y4[:], ALU.add)
 
         blocks = BANK // P

from contextlib import ExitStack

import concourse.mybir as mybir
from concourse.masks import make_identity

D, E, T, Q, SLOTS = 512, 512, 1024, 128, 512
FLOPS = 3 * 2 * 512 * 128 * 1024

F32 = mybir.dt.float32
BF16 = mybir.dt.bfloat16
I32 = mybir.dt.int32
U32 = mybir.dt.uint32
U16 = mybir.dt.uint16
U8 = mybir.dt.uint8
FP8X4 = mybir.dt.float8_e4m3fn_x4
FP4X4 = mybir.dt.float4_e2m1fn_x4
ALU = mybir.AluOpType
ACT = mybir.ActivationFunctionType

P = 128
PACK = 4
BANK = 512
CHUNK = 256
OUT_SCALE = 512.0


def tile_attend_hvproductpairs_heads_kernel(tc, query, keys_words, keys_scales, gout, vals, dquery, base, offs, offs2, out):
    nc = tc.nc
    with ExitStack() as ctx:
        sb = ctx.enter_context(tc.tile_pool(name="sb", bufs=1))
        shared = ctx.enter_context(tc.tile_pool(name="shared", bufs=1))
        ps = ctx.enter_context(tc.psum_pool(name="ps", bufs=1))

        def load_rows(name, rows, raw=None):
            if raw is None:
                raw = sb.tile([P, PACK, rows.shape[1]], F32, name=name + "_raw", align_bytes=64)
            nc.sync.dma_start(out=raw[:], in_=rows.rearrange("(p j) w -> p j w", j=PACK))
            return raw

        def weave(copy, grouped, raw):
            copy(out=grouped.rearrange("p (c i j) -> p c j i", i=4, j=PACK),
                 in_=raw.rearrange("p j (c i) -> p c j i", i=4))

        def interleave(name, raw, copy):
            width = raw.shape[2]
            grouped = sb.tile([P, width * PACK], BF16, name=name + "_bf", align_bytes=64)
            weave(copy, grouped[:], raw[:])
            return grouped

        def quantize(name, grouped):
            width = grouped.shape[1] // PACK
            codes = sb.tile([P, width], U32, name=name + "_codes", align_bytes=64)
            scales = sb.tile([P, width], U8, name=name + "_scales", align_bytes=64)
            nc.vector.quantize_mx(out=codes[:].bitcast(FP8X4), scales=scales[:], in_=grouped[:])
            return codes, scales

        def wide(name, on=None):
            return sb.tile([P, SLOTS], F32, name=name, tag=on or name, align_bytes=64)

        def column(name):
            return sb.tile([P, 1], F32, name=name)

        k_scales = sb.tile([P, T], U8, name="k_scales", align_bytes=64)
        nc.vector.memset(k_scales[:].bitcast(U32), 0)
        q_raw = load_rows("q", query)
        k_words = sb.tile([P, 2 * T], U8, name="k_words", align_bytes=64)
        nc.sync.dma_start(out=k_words[:].bitcast(I32), in_=keys_words[0].bitcast(I32))
        for quad in range(4):
            nc.sync.dma_start(out=k_scales[32 * quad:32 * quad + 4, :].bitcast(I32),
                              in_=keys_scales[0, 4 * quad:4 * quad + 4, :].bitcast(I32))
        dq_raw = load_rows("dq", dquery)
        g_raw = load_rows("g", gout)
        list1 = sb.tile([P, SLOTS // 16], U16, name="list1")
        nc.sync.dma_start(list1[:], offs)
        list2 = sb.tile([P, SLOTS // 16], U16, name="list2")
        nc.sync.dma_start(list2[:], offs2)
        v_cols = [(0, 256), (256, 512), (512, 768), (768, 896), (896, 1024)]
        v_raw = [load_rows("v%d" % c, vals[:, lo:hi]) for c, (lo, hi) in enumerate(v_cols[:-1])]
        v_last = shared.tile([P, PACK, P], F32, name="v_last", offset=2 * SLOTS)
        v_raw.append(load_rows("v4", vals[:, T - P:T], v_last))
        base_sb = sb.tile([P, T], F32, name="base_sb")
        nc.sync.dma_start(out=base_sb[:], in_=base)

        placed1 = sb.tile([P, T], F32, name="placed1")
        placed2 = sb.tile([P, T], F32, name="placed2")
        nc.vector.memset(placed1[:], 0.0)
        nc.gpsimd.memset(placed2[:], 0.0)
        ident = sb.tile([P, P], F32, name="ident")
        make_identity(nc, ident[:])

        def score_keys(name, codes, scales, width, copies):
            whole = sb.tile([P, T], F32, name=name)
            for h in range(T // width):
                bank = ps.tile([P, width], F32, name="%s_bank%d" % (name, h))
                nc.tensor.matmul_mx(out=bank[:], lhsT=codes[:].bitcast(FP8X4), lhsT_scale=scales[:],
                                    rhs=k_words[:, 2 * width * h:2 * width * (h + 1)].bitcast(FP4X4),
                                    rhs_scale=k_scales[:, width * h:width * (h + 1)], start=True, stop=True)
                copies[h % len(copies)](out=whole[:, width * h:width * (h + 1)], in_=bank[:])
            return whole

        q_bf = sb.tile([P, Q * PACK], BF16, name="q_bf", align_bytes=64)
        q_codes = sb.tile([P, Q], U32, name="q_codes", align_bytes=64)
        q_scales = sb.tile([P, Q], U8, name="q_scales", align_bytes=64)
        halves = [(0, Q // 2), (Q // 2, Q)]
        for lo, hi in halves:
            weave(nc.vector.tensor_copy, q_bf[:, PACK * lo:PACK * hi], q_raw[:, :, lo:hi])
        for lo, hi in halves:
            nc.vector.quantize_mx(out=q_codes[:, lo:hi].bitcast(FP8X4), scales=q_scales[:, lo:hi], in_=q_bf[:, PACK * lo:PACK * hi])
        a = score_keys("a", q_codes, q_scales, CHUNK, [nc.scalar.copy])
        dq_codes, dq_scales = quantize("dq", interleave("dq", dq_raw, nc.vector.tensor_copy))
        ta = score_keys("ta", dq_codes, dq_scales, BANK, [nc.scalar.copy])
        g_codes, g_scales = quantize("g", interleave("g", g_raw, nc.vector.tensor_copy))

        u1, u2, s, t1, t2 = wide("u1"), wide("u2"), wide("s"), wide("t1"), wide("t2")
        neg_max, z, rz, neg_r = column("neg_max"), column("z"), column("rz"), column("neg_r")
        nc.vector.tensor_scalar(u1[:], a[:].indirect(list1[:]), 1.0, 0.5, ALU.mult, ALU.add)
        nc.vector.tensor_scalar(u2[:], a[:].indirect(list2[:]), 1.0, 0.5, ALU.mult, ALU.add)
        nc.vector.tensor_copy(t1[:], ta[:].indirect(list1[:]))
        nc.vector.tensor_copy(t2[:], ta[:].indirect(list2[:]))
        v_first = sb.tile([P, BANK * PACK], BF16, name="v_first", tag="g_bf", align_bytes=64)
        nc.gpsimd.tensor_scalar(v_first[:, :CHUNK * PACK].rearrange("p (w j) -> p w j", j=PACK),
                                v_raw[0][:].rearrange("p j w -> p w j"), 1.0, 0.0, ALU.mult, ALU.add)
        x1 = wide("x1")
        nc.gpsimd.tensor_tensor(s[:], u1[:], u2[:], ALU.mult)
        nc.gpsimd.tensor_tensor(x1[:], t1[:], u2[:], ALU.mult)
        nc.vector.tensor_reduce(neg_max[:], s[:], mybir.AxisListType.X, ALU.max, negate=True)

        weave(nc.scalar.copy, v_first[:, CHUNK * PACK:], v_raw[1][:])
        v_bf = [v_first] + [interleave("v%d" % c, v_raw[c], nc.scalar.copy) for c in range(2, len(v_cols))]
        p = shared.tile([P, SLOTS], F32, name="p", offset=0)
        nc.scalar.activation(p[:], s[:], ACT.Exp, bias=neg_max[:], scale=1.0, accum_out=z[:])
        nc.vector.reciprocal(rz[:], z[:])

        c0 = shared.tile([P, T], F32, name="c0", offset=4 * SLOTS)
        lo = 0
        for c, grouped in enumerate(v_bf):
            width = grouped.shape[1] // PACK
            v_codes, v_scales = quantize("vq%d" % c, grouped)
            bank = ps.tile([P, width], F32, name="c0_bank%d" % c, tag="a_bank%d" % c)
            nc.tensor.matmul_mx(out=bank[:], lhsT=g_codes[:].bitcast(FP8X4), lhsT_scale=g_scales[:],
                                rhs=v_codes[:].bitcast(FP8X4), rhs_scale=v_scales[:], start=True, stop=True)
            nc.scalar.copy(out=c0[:, lo:lo + width], in_=bank[:])
            lo = lo + width

        w = wide("w", on="vq3_codes")
        nc.scalar.activation(w[:], p[:], ACT.Copy, scale=rz[:])
        nc.scalar.activation(neg_r[:], rz[:], ACT.Copy, scale=-OUT_SCALE)

        x2, neg_xs = wide("x2", on="v4_bf"), wide("neg_xs")
        nc.vector.tensor_tensor(x2[:], t2[:], u1[:], ALU.mult)
        nc.vector.scalar_tensor_tensor(neg_xs[:], x1[:], -1.0, x2[:], ALU.mult, ALU.subtract)

        pdw, neg_wdw, neg_wxs = wide("pdw"), wide("neg_wdw"), wide("neg_wxs")
        neg_m, neg_mx, neg_cov = column("neg_m"), column("neg_mx"), column("neg_cov")
        nc.vector.tensor_tensor(pdw[:], c0[:].indirect(list1[:]), p[:], ALU.mult)
        nc.scalar.activation(neg_wdw[:], pdw[:], ACT.Copy, scale=neg_r[:], accum_out=neg_m[:])
        nc.vector.scalar_tensor_tensor(neg_wxs[:], neg_xs[:], 1.0, w[:], ALU.mult, ALU.mult, accum_out=neg_mx[:])

        ds, neg_c, xds = wide("ds"), wide("neg_c"), wide("xds")
        y1, y2, e1 = wide("y1"), wide("y2"), wide("e1")
        half = SLOTS // 2
        for lo in (0, half):
            nc.vector.scalar_tensor_tensor(ds[:, lo:lo + half], w[:, lo:lo + half], neg_m[:], neg_wdw[:, lo:lo + half],
                                           ALU.mult, ALU.subtract)
        nc.vector.tensor_tensor(y2[:, :half], ds[:, :half], t2[:, :half], ALU.mult)
        nc.vector.scalar_tensor_tensor(neg_c[:], neg_xs[:], neg_mx[:], ds[:], ALU.subtract, ALU.mult, accum_out=neg_cov[:])
        nc.vector.tensor_tensor(y2[:, half:], ds[:, half:], t2[:, half:], ALU.mult)
        halves = [slice(0, half), slice(half, SLOTS)]
        for cols in halves:
            nc.vector.scalar_tensor_tensor(xds[:, cols], w[:, cols], neg_cov[:], neg_c[:, cols], ALU.mult, ALU.subtract)
        for cols in halves:
            nc.vector.tensor_tensor(y1[:, cols], xds[:, cols], u2[:, cols], ALU.mult)
        for cols in halves:
            nc.vector.tensor_tensor(e1[:, cols], y1[:, cols], y2[:, cols], ALU.add)
        nc.vector.tensor_copy(placed1[:].indirect(list1[:]), e1[:])
        y3, y4 = wide("y3", on="y1"), wide("y4", on="y2")
        nc.gpsimd.tensor_tensor(y4[:], ds[:], t1[:], ALU.mult)
        nc.gpsimd.tensor_tensor(y3[:], xds[:], u1[:], ALU.mult)
        nc.vector.tensor_tensor(placed2[:].indirect(list2[:]), y3[:], y4[:], ALU.add)

        blocks = BANK // P
        for h in range(T // BANK):
            turned = ps.tile([P, BANK], F32, name="turned%d" % h, tag="ta_bank%d" % h)
            for i, src in enumerate((base_sb, placed1)):
                for b in range(blocks):
                    lo = BANK * h + P * b
                    nc.tensor.matmul(turned[:, P * b:P * (b + 1)], src[:, lo:lo + P], ident[:], is_transpose=True,
                                     start=(i == 0 and b == 0), stop=(i == 1 and b == blocks - 1))
            turned_sb = sb.tile([P, BANK], F32, name="turned_sb%d" % h)
            nc.scalar.copy(out=turned_sb[:], in_=turned[:])
            back = ps.tile([P, BANK], F32, name="back%d" % h)
            for b in range(blocks):
                nc.tensor.transpose(back[:, P * b:P * (b + 1)], turned_sb[:, P * b:P * (b + 1)], ident[:])
            for lo in (0, CHUNK):
                cols = slice(BANK * h + lo, BANK * h + lo + CHUNK)
                result = sb.tile([P, CHUNK], F32, name="result%d" % cols.start)
                nc.vector.tensor_tensor(result[:], back[:, lo:lo + CHUNK], placed2[:, cols], ALU.add)
                (nc.sync if lo == 0 else nc.scalar).dma_start(out=out[:, cols], in_=result[:])
